import numpy as np
import ml_dtypes


def mxq(x, axis, fmt="e4m3"):
    dtype, down = {"e4m3": (ml_dtypes.float8_e4m3fn, 7), "e5m2": (ml_dtypes.float8_e5m2, 14)}[fmt]
    v = np.moveaxis(np.asarray(x, np.float32).astype(ml_dtypes.bfloat16).astype(np.float64), axis, -1)
    blocks = v.reshape(v.shape[:-1] + (-1, 32))
    amax = np.abs(blocks).max(-1, keepdims=True)
    byte = np.maximum(np.where(amax > 0, np.frexp(amax)[1] - 1 + 127, 0) - down, 1)
    scale = np.exp2(byte - 127.0)
    codes = (blocks / scale).astype(np.float32).astype(dtype).astype(np.float64)
    return np.moveaxis((codes * scale).reshape(v.shape), -1, axis)


WIDE = False


def mx_kscale(k):
    if not WIDE:
        return np.ones(k)
    levels = np.array([10, -10, 5, -5, 0])
    if k % 512:
        return np.exp2(np.random.permutation(np.resize(levels, k // 32))).repeat(32)
    a = np.empty((k // 512, 16))
    for p in range(k // 512):
        a[p, :8] = np.random.permutation(np.resize(levels, 8))
        for g in range(8):
            far = levels[np.abs(levels - a[p, g]) >= 10]
            a[p, g + 8] = far[np.random.randint(len(far))]
    return np.exp2(a.ravel()).repeat(32)


def f64(x):
    return np.asarray(x).astype(np.float64)


def striped(idx):
    return np.tile(idx.reshape(-1, 16).T, (8, 1)).astype(np.uint16)


def unstriped(offs):
    return offs[:16].T.reshape(-1).astype(np.int64)


def silu(v):
    return v / (1.0 + np.exp(-np.maximum(v, -700.0)))


K, T, E, C, N = 1536, 2048, 8, 256, 128


def by_expert(wq, xq):
    return np.concatenate([wq[e].T @ xq[:, e * C:(e + 1) * C] for e in range(E)], axis=1)


def setup_inputs():
    n = np.random.standard_normal
    s = mx_kscale(K)[:, None]
    return {
        "xT": (n((K, T)) * s).astype(np.float32),
        "w": (n((E, K, N)) / np.sqrt(K) / s[None]).astype(np.float32),
        "b": (0.3 * n((N, E))).astype(np.float32),
        "gate": np.tile(np.random.uniform(0.2, 1.0, E * C), (N, 1)).astype(np.float32),
        "offs": striped(np.random.permutation(T)[:E * C]),
    }


def reference(xT, w, b, gate, offs):
    idx = unstriped(offs)
    xq = mxq(f64(xT)[:, idx], 0, "e4m3")
    y = by_expert(mxq(f64(w), 1, "e4m3"), xq)
    y = silu(y + np.repeat(f64(b), C, axis=1))
    out = np.zeros((N, T))
    out[:, idx] = f64(gate) * y
    return out

@@ -1,0 +1,153 @@
+import concourse.mybir as mybir
+
+K, T, E, C, N = 1536, 2048, 8, 256, 128
+FLOPS = 2 * K * E * C * N
+
+P = 128
+PACK = 4
+K_PASS = P * PACK
+PASSES = K // K_PASS
+SUB = 512
+STRIPE = 16
+
+F32 = mybir.dt.float32
+BF16 = mybir.dt.bfloat16
+U32 = mybir.dt.uint32
+U16 = mybir.dt.uint16
+U8 = mybir.dt.uint8
+FP8X4 = mybir.dt.float8_e4m3fn_x4
+MULT = mybir.AluOpType.mult
+SILU = mybir.ActivationFunctionType.Silu
+
+LOADS = ((1024, 1024), (1024, 1024), (1024, 512, 512))
+SCALAR_TOKENS = ((512, 0, 512, 512), (512, 0, 512, 512), (512, 384, 192, 192))
+
+
+def tile_routed_moe_kernel(tc, xT, w, b, gate, offs, out):
+    nc = tc.nc
+
+    def interleave(engine_copy, dst, src):
+        engine_copy(
+            out=dst.rearrange("p (c i) t -> p c t i", i=4),
+            in_=src.rearrange("p t (c i) -> p c t i", i=4),
+        )
+
+    with (
+        tc.tile_pool(name="keep", bufs=1) as keep,
+        tc.tile_pool(name="raw", bufs=4) as raw_pool,
+        tc.tile_pool(name="group", bufs=4) as group_pool,
+        tc.tile_pool(name="wgroup", bufs=3) as wgroup_pool,
+        tc.tile_pool(name="ys", bufs=4) as y_pool,
+        tc.psum_pool(name="psum", bufs=8) as psum_pool,
+    ):
+        offsets = keep.tile([P, E * C // STRIPE], U16, name="offsets")
+        bias = keep.tile([P, E], F32, name="bias")
+        gates = keep.tile([P, E * C], F32, name="gates")
+        window = keep.tile([P, T], F32, name="window")
+        x_words = [keep.tile([P, T], U32, name=f"x_words{a}", align_bytes=64) for a in range(PASSES)]
+        x_scales = keep.tile([P, T], U8, name="x_scales", align_bytes=64)
+        g_words = keep.tile([P, PASSES, E * C], U32, name="g_words", align_bytes=64)
+        g_scales = keep.tile([P, E * C], U8, name="g_scales", align_bytes=64)
+        w_words = keep.tile([P, E, PASSES, N], U32, name="w_words", align_bytes=64)
+        w_scales = keep.tile([P, E, PASSES, N], U8, name="w_scales", align_bytes=64)
+        warm = keep.tile([P, 1], F32, name="warm")
+
+        nc.gpsimd.memset(x_scales[:], 0)
+        nc.gpsimd.memset(warm[:], 0.0)
+        nc.scalar.activation(out=warm[:], in_=warm[:], func=SILU)
+
+        def gather(dst, src, lo, hi):
+            nc.vector.tensor_copy(out=dst[:, lo:hi], in_=src[:].indirect(offsets[:, lo // STRIPE : hi // STRIPE]))
+
+        first = True
+        for a in range(PASSES):
+            planes = xT[a * K_PASS : (a + 1) * K_PASS, :].rearrange("(p t) n -> p t n", t=PACK)
+            t0 = 0
+            for width in LOADS[a]:
+                raw = raw_pool.tile([P, PACK, width], F32, name="raw", tag="raw")
+                nc.sync.dma_start(out=raw[:], in_=planes[:, :, t0 : t0 + width])
+                if first:
+                    nc.sync.dma_start(out=offsets[:], in_=offs)
+                    nc.sync.dma_start(out=bias[:], in_=b)
+                    first = False
+                for s in range(0, width, SUB):
+                    grouped = group_pool.tile([P, SUB, PACK], BF16, name="grouped", align_bytes=64)
+                    split = SCALAR_TOKENS[a][(t0 + s) // SUB]
+                    if split > 0:
+                        interleave(nc.scalar.copy, grouped[:, :split, :], raw[:, :, s : s + split])
+                    if split < SUB:
+                        interleave(nc.vector.tensor_copy, grouped[:, split:, :], raw[:, :, s + split : s + SUB])
+                    nc.vector.quantize_mx(
+                        out=x_words[a][:, t0 + s : t0 + s + SUB].bitcast(FP8X4),
+                        scales=x_scales[4 * a :, t0 + s : t0 + s + SUB],
+                        in_=grouped[:].rearrange("p c t -> p (c t)"),
+                    )
+                t0 += width
+            if a < PASSES - 1:
+                for lo in range(0, E * C, 1024):
+                    gather(g_words[:, a, :], x_words[a], lo, lo + 1024)
+
+        w_raws = []
+        for e in range(E):
+            w_raw = keep.tile([P, PASSES, PACK, N], F32, name=f"w_raw{e}")
+            nc.sync.dma_start(
+                out=w_raw[:].rearrange("p a t n -> p a (t n)"),
+                in_=w[e].rearrange("(a p t) n -> p a (t n)", p=P, t=PACK),
+            )
+            w_raws.append(w_raw)
+            if e == 1:
+                nc.sync.dma_start(out=gates[:], in_=gate)
+
+        def weights(e):
+            grouped = wgroup_pool.tile([P, PASSES, N, PACK], BF16, name="w_grouped", align_bytes=64)
+            nc.scalar.copy(
+                out=grouped[:].rearrange("p a (c i) t -> p a c t i", i=4),
+                in_=w_raws[e][:].rearrange("p a t (c i) -> p a c t i", i=4),
+            )
+            for a0, a1 in ((0, 2), (2, 3)):
+                nc.vector.quantize_mx(
+                    out=w_words[:, e, a0:a1, :].rearrange("p a n -> p (a n)").bitcast(FP8X4),
+                    scales=w_scales[:, e, a0:a1, :].rearrange("p a n -> p (a n)"),
+                    in_=grouped[:, a0:a1].rearrange("p a n t -> p (a n t)"),
+                )
+
+        def multiply(e):
+            slots = slice(e * C, (e + 1) * C)
+            acc = psum_pool.tile([P, C], F32, name="acc")
+            for a in range(PASSES):
+                nc.tensor.matmul_mx(
+                    out=acc[:],
+                    lhsT=w_words[:, e, a, :].bitcast(FP8X4),
+                    lhsT_scale=w_scales[:, e, a, :],
+                    rhs=g_words[:, a, slots].bitcast(FP8X4),
+                    rhs_scale=g_scales[4 * a :, slots],
+                    start=(a == 0),
+                    stop=(a == PASSES - 1),
+                )
+            y = y_pool.tile([P, C], F32, name="y")
+            nc.scalar.activation(out=y[:], in_=acc[:], func=SILU, bias=bias[:, e : e + 1])
+            z = y_pool.tile([P, C], F32, name="z")
+            nc.gpsimd.tensor_tensor(out=z[:], in0=y[:], in1=gates[:, slots], op=MULT)
+            return z
+
+        def scatter(e, z):
+            nc.vector.tensor_copy(
+                out=window[:].indirect(offsets[:, e * C // STRIPE : (e + 1) * C // STRIPE]), in_=z[:]
+            )
+
+        weights(0)
+        weights(1)
+        pending = []
+        for pair in range(E // 2):
+            lo, hi = pair * 2 * C, (pair + 1) * 2 * C
+            gather(g_words[:, PASSES - 1, :], x_words[PASSES - 1], lo, hi)
+            gather(g_scales, x_scales, lo, hi)
+            for e in (2 * pair, 2 * pair + 1):
+                pending.append((e, multiply(e)))
+                if e + 2 < E:
+                    weights(e + 2)
+                if len(pending) > 2:
+                    scatter(*pending.pop(0))
+        for e, z in pending:
+            scatter(e, z)
+        nc.sync.dma_start(out=out, in_=window[:])

@@ -19,8 +19,9 @@ FP8X4 = mybir.dt.float8_e4m3fn_x4
 MULT = mybir.AluOpType.mult
 SILU = mybir.ActivationFunctionType.Silu
 
-LOADS = ((1024, 1024), (1024, 1024), (1024, 512, 512))
-SCALAR_TOKENS = ((512, 0, 512, 512), (512, 0, 512, 512), (512, 384, 192, 192))
+HALF = 1024
+LOADS = ((SUB, SUB), (HALF,), (HALF,), (HALF,), (HALF,), (SUB, SUB))
+SCALAR_TOKENS = ((512, 128, 512, 384), (512, 512, 512, 384), (512, 384, 384, 208))
 
 
 def tile_routed_moe_kernel(tc, xT, w, b, gate, offs, out):
@@ -34,10 +35,10 @@ def tile_routed_moe_kernel(tc, xT, w, b, gate, offs, out):
 
     with (
         tc.tile_pool(name="keep", bufs=1) as keep,
-        tc.tile_pool(name="raw", bufs=4) as raw_pool,
+        tc.tile_pool(name="raw", bufs=6) as raw_pool,
         tc.tile_pool(name="group", bufs=4) as group_pool,
-        tc.tile_pool(name="wgroup", bufs=3) as wgroup_pool,
-        tc.tile_pool(name="ys", bufs=4) as y_pool,
+        tc.tile_pool(name="wgroup", bufs=2) as wgroup_pool,
+        tc.tile_pool(name="ys", bufs=3) as y_pool,
         tc.psum_pool(name="psum", bufs=8) as psum_pool,
     ):
         offsets = keep.tile([P, E * C // STRIPE], U16, name="offsets")
@@ -62,15 +63,18 @@ def tile_routed_moe_kernel(tc, xT, w, b, gate, offs, out):
         first = True
         for a in range(PASSES):
             planes = xT[a * K_PASS : (a + 1) * K_PASS, :].rearrange("(p t) n -> p t n", t=PACK)
-            t0 = 0
-            for width in LOADS[a]:
-                raw = raw_pool.tile([P, PACK, width], F32, name="raw", tag="raw")
-                nc.sync.dma_start(out=raw[:], in_=planes[:, :, t0 : t0 + width])
+            for half in range(T // HALF):
+                t0 = half * HALF
+                raw = raw_pool.tile([P, PACK, HALF], F32, name="raw", tag="raw")
+                c0 = 0
+                for width in LOADS[2 * a + half]:
+                    nc.sync.dma_start(out=raw[:, :, c0 : c0 + width], in_=planes[:, :, t0 + c0 : t0 + c0 + width])
+                    c0 += width
                 if first:
                     nc.sync.dma_start(out=offsets[:], in_=offs)
                     nc.sync.dma_start(out=bias[:], in_=b)
                     first = False
-                for s in range(0, width, SUB):
+                for s in range(0, HALF, SUB):
                     grouped = group_pool.tile([P, SUB, PACK], BF16, name="grouped", align_bytes=64)
                     split = SCALAR_TOKENS[a][(t0 + s) // SUB]
                     if split > 0:
@@ -82,72 +86,83 @@ def tile_routed_moe_kernel(tc, xT, w, b, gate, offs, out):
                         scales=x_scales[4 * a :, t0 + s : t0 + s + SUB],
                         in_=grouped[:].rearrange("p c t -> p (c t)"),
                     )
-                t0 += width
             if a < PASSES - 1:
                 for lo in range(0, E * C, 1024):
                     gather(g_words[:, a, :], x_words[a], lo, lo + 1024)
 
+        nc.sync.dma_start(out=gates[:], in_=gate)
         w_raws = []
-        for e in range(E):
-            w_raw = keep.tile([P, PASSES, PACK, N], F32, name=f"w_raw{e}")
-            nc.sync.dma_start(
-                out=w_raw[:].rearrange("p a t n -> p a (t n)"),
-                in_=w[e].rearrange("(a p t) n -> p a (t n)", p=P, t=PACK),
-            )
-            w_raws.append(w_raw)
-            if e == 1:
-                nc.sync.dma_start(out=gates[:], in_=gate)
+        for pair in range(E // 2):
+            w_pair = raw_pool.tile([P, 2, PASSES, PACK, N], F32, name="w_pair", tag="raw")
+            for i in range(2):
+                nc.sync.dma_start(
+                    out=w_pair[:, i].rearrange("p a t n -> p a (t n)"),
+                    in_=w[2 * pair + i].rearrange("(a p t) n -> p a (t n)", p=P, t=PACK),
+                )
+            w_raws.append(w_pair)
 
-        def weights(e):
-            grouped = wgroup_pool.tile([P, PASSES, N, PACK], BF16, name="w_grouped", align_bytes=64)
+        def weights(pair):
+            experts = slice(2 * pair, 2 * pair + 2)
+            grouped = wgroup_pool.tile([P, 2 * PASSES, N, PACK], BF16, name="w_grouped", align_bytes=64)
             nc.scalar.copy(
                 out=grouped[:].rearrange("p a (c i) t -> p a c t i", i=4),
-                in_=w_raws[e][:].rearrange("p a t (c i) -> p a c t i", i=4),
+                in_=w_raws[pair][:].rearrange("p e a t (c i) -> p (e a) c t i", i=4),
             )
-            for a0, a1 in ((0, 2), (2, 3)):
+            words = w_words[:, experts].rearrange("p e a n -> p (e a n)")
+            scales = w_scales[:, experts].rearrange("p e a n -> p (e a n)")
+            values = grouped[:].rearrange("p a n t -> p (a n t)")
+            for lo, hi in ((0, 4 * N), (4 * N, 6 * N)):
                 nc.vector.quantize_mx(
-                    out=w_words[:, e, a0:a1, :].rearrange("p a n -> p (a n)").bitcast(FP8X4),
-                    scales=w_scales[:, e, a0:a1, :].rearrange("p a n -> p (a n)"),
-                    in_=grouped[:, a0:a1].rearrange("p a n t -> p (a n t)"),
+                    out=words[:, lo:hi].bitcast(FP8X4), scales=scales[:, lo:hi], in_=values[:, PACK * lo : PACK * hi]
                 )
 
-        def multiply(e):
-            slots = slice(e * C, (e + 1) * C)
-            acc = psum_pool.tile([P, C], F32, name="acc")
-            for a in range(PASSES):
-                nc.tensor.matmul_mx(
-                    out=acc[:],
-                    lhsT=w_words[:, e, a, :].bitcast(FP8X4),
-                    lhsT_scale=w_scales[:, e, a, :],
-                    rhs=g_words[:, a, slots].bitcast(FP8X4),
-                    rhs_scale=g_scales[4 * a :, slots],
-                    start=(a == 0),
-                    stop=(a == PASSES - 1),
-                )
-            y = y_pool.tile([P, C], F32, name="y")
-            nc.scalar.activation(out=y[:], in_=acc[:], func=SILU, bias=bias[:, e : e + 1])
-            z = y_pool.tile([P, C], F32, name="z")
-            nc.gpsimd.tensor_tensor(out=z[:], in0=y[:], in1=gates[:, slots], op=MULT)
+        def multiply(pair):
+            y = y_pool.tile([P, 2 * C], F32, name="y")
+            z = y_pool.tile([P, 2 * C], F32, name="z")
+            for i in range(2):
+                e = 2 * pair + i
+                slots = slice(e * C, (e + 1) * C)
+                acc = psum_pool.tile([P, C], F32, name="acc")
+                for a in range(PASSES):
+                    nc.tensor.matmul_mx(
+                        out=acc[:],
+                        lhsT=w_words[:, e, a, :].bitcast(FP8X4),
+                        lhsT_scale=w_scales[:, e, a, :],
+                        rhs=g_words[:, a, slots].bitcast(FP8X4),
+                        rhs_scale=g_scales[4 * a :, slots],
+                        start=(a == 0),
+                        stop=(a == PASSES - 1),
+                    )
+                here = slice(i * C, (i + 1) * C)
+                nc.scalar.activation(out=y[:, here], in_=acc[:], func=SILU, bias=bias[:, e : e + 1])
+                nc.gpsimd.tensor_tensor(out=z[:, here], in0=y[:, here], in1=gates[:, slots], op=MULT)
             return z
 
-        def scatter(e, z):
-            nc.vector.tensor_copy(
-                out=window[:].indirect(offsets[:, e * C // STRIPE : (e + 1) * C // STRIPE]), in_=z[:]
-            )
+        def scatter(pair, z):
+            step = C if pair == E // 2 - 1 else 2 * C
+            for lo in range(0, 2 * C, step):
+                first = pair * 2 * C + lo
+                nc.vector.tensor_copy(
+                    out=window[:].indirect(offsets[:, first // STRIPE : (first + step) // STRIPE]),
+                    in_=z[:, lo : lo + step],
+                )
 
-        weights(0)
-        weights(1)
-        pending = []
-        for pair in range(E // 2):
-            lo, hi = pair * 2 * C, (pair + 1) * 2 * C
+        def late_gathers(lo, hi):
             gather(g_words[:, PASSES - 1, :], x_words[PASSES - 1], lo, hi)
             gather(g_scales, x_scales, lo, hi)
-            for e in (2 * pair, 2 * pair + 1):
-                pending.append((e, multiply(e)))
-                if e + 2 < E:
-                    weights(e + 2)
-                if len(pending) > 2:
-                    scatter(*pending.pop(0))
-        for e, z in pending:
-            scatter(e, z)
+
+        late_gathers(0, 1024)
+        weights(0)
+        weights(1)
+        z0 = multiply(0)
+        z1 = multiply(1)
+        late_gathers(1024, 2048)
+        scatter(0, z0)
+        weights(2)
+        z2 = multiply(2)
+        scatter(1, z1)
+        weights(3)
+        z3 = multiply(3)
+        scatter(2, z2)
+        scatter(3, z3)
         nc.sync.dma_start(out=out, in_=window[:])

@@ -21,7 +21,7 @@ SILU = mybir.ActivationFunctionType.Silu
 
 HALF = 1024
 LOADS = ((SUB, SUB), (HALF,), (HALF,), (HALF,), (HALF,), (SUB, SUB))
-SCALAR_TOKENS = ((512, 128, 512, 384), (512, 512, 512, 384), (512, 384, 384, 208))
+SCALAR_TOKENS = ((512, 0, 512, 0), (512, 256, 512, 256), (512, 128, 256, 160))
 
 
 def tile_routed_moe_kernel(tc, xT, w, b, gate, offs, out):
@@ -38,6 +38,7 @@ def tile_routed_moe_kernel(tc, xT, w, b, gate, offs, out):
         tc.tile_pool(name="raw", bufs=6) as raw_pool,
         tc.tile_pool(name="group", bufs=4) as group_pool,
         tc.tile_pool(name="wgroup", bufs=2) as wgroup_pool,
+        tc.tile_pool(name="late", bufs=3) as late_pool,
         tc.tile_pool(name="ys", bufs=3) as y_pool,
         tc.psum_pool(name="psum", bufs=8) as psum_pool,
     ):
@@ -47,7 +48,7 @@ def tile_routed_moe_kernel(tc, xT, w, b, gate, offs, out):
         window = keep.tile([P, T], F32, name="window")
         x_words = [keep.tile([P, T], U32, name=f"x_words{a}", align_bytes=64) for a in range(PASSES)]
         x_scales = keep.tile([P, T], U8, name="x_scales", align_bytes=64)
-        g_words = keep.tile([P, PASSES, E * C], U32, name="g_words", align_bytes=64)
+        g_words = keep.tile([P, PASSES - 1, E * C], U32, name="g_words", align_bytes=64)
         g_scales = keep.tile([P, E * C], U8, name="g_scales", align_bytes=64)
         w_words = keep.tile([P, E, PASSES, N], U32, name="w_words", align_bytes=64)
         w_scales = keep.tile([P, E, PASSES, N], U8, name="w_scales", align_bytes=64)
@@ -58,7 +59,7 @@ def tile_routed_moe_kernel(tc, xT, w, b, gate, offs, out):
         nc.scalar.activation(out=warm[:], in_=warm[:], func=SILU)
 
         def gather(dst, src, lo, hi):
-            nc.vector.tensor_copy(out=dst[:, lo:hi], in_=src[:].indirect(offsets[:, lo // STRIPE : hi // STRIPE]))
+            nc.vector.tensor_copy(out=dst, in_=src[:].indirect(offsets[:, lo // STRIPE : hi // STRIPE]))
 
         first = True
         for a in range(PASSES):
@@ -88,9 +89,8 @@ def tile_routed_moe_kernel(tc, xT, w, b, gate, offs, out):
                     )
             if a < PASSES - 1:
                 for lo in range(0, E * C, 1024):
-                    gather(g_words[:, a, :], x_words[a], lo, lo + 1024)
+                    gather(g_words[:, a, lo : lo + 1024], x_words[a], lo, lo + 1024)
 
-        nc.sync.dma_start(out=gates[:], in_=gate)
         w_raws = []
         for pair in range(E // 2):
             w_pair = raw_pool.tile([P, 2, PASSES, PACK, N], F32, name="w_pair", tag="raw")
@@ -100,6 +100,8 @@ def tile_routed_moe_kernel(tc, xT, w, b, gate, offs, out):
                     in_=w[2 * pair + i].rearrange("(a p t) n -> p a (t n)", p=P, t=PACK),
                 )
             w_raws.append(w_pair)
+            if pair == 1:
+                nc.sync.dma_start(out=gates[:], in_=gate)
 
         def weights(pair):
             experts = slice(2 * pair, 2 * pair + 2)
@@ -116,53 +118,56 @@ def tile_routed_moe_kernel(tc, xT, w, b, gate, offs, out):
                     out=words[:, lo:hi].bitcast(FP8X4), scales=scales[:, lo:hi], in_=values[:, PACK * lo : PACK * hi]
                 )
 
-        def multiply(pair):
+        def late_words(pair):
+            words = late_pool.tile([P, 2 * C], U32, name="late", align_bytes=64)
+            gather(words[:], x_words[PASSES - 1], pair * 2 * C, (pair + 1) * 2 * C)
+            return words
+
+        def multiply(pair, late):
             y = y_pool.tile([P, 2 * C], F32, name="y")
-            z = y_pool.tile([P, 2 * C], F32, name="z")
             for i in range(2):
                 e = 2 * pair + i
                 slots = slice(e * C, (e + 1) * C)
+                here = slice(i * C, (i + 1) * C)
                 acc = psum_pool.tile([P, C], F32, name="acc")
                 for a in range(PASSES):
+                    words = late[:, here] if a == PASSES - 1 else g_words[:, a, slots]
                     nc.tensor.matmul_mx(
                         out=acc[:],
                         lhsT=w_words[:, e, a, :].bitcast(FP8X4),
                         lhsT_scale=w_scales[:, e, a, :],
-                        rhs=g_words[:, a, slots].bitcast(FP8X4),
+                        rhs=words.bitcast(FP8X4),
                         rhs_scale=g_scales[4 * a :, slots],
                         start=(a == 0),
                         stop=(a == PASSES - 1),
                     )
-                here = slice(i * C, (i + 1) * C)
                 nc.scalar.activation(out=y[:, here], in_=acc[:], func=SILU, bias=bias[:, e : e + 1])
-                nc.gpsimd.tensor_tensor(out=z[:, here], in0=y[:, here], in1=gates[:, slots], op=MULT)
-            return z
+            return y
 
-        def scatter(pair, z):
-            step = C if pair == E // 2 - 1 else 2 * C
+        def scatter(pair, y, step):
             for lo in range(0, 2 * C, step):
-                first = pair * 2 * C + lo
-                nc.vector.tensor_copy(
-                    out=window[:].indirect(offsets[:, first // STRIPE : (first + step) // STRIPE]),
-                    in_=z[:, lo : lo + step],
+                slot = pair * 2 * C + lo
+                nc.vector.tensor_tensor(
+                    out=window[:].indirect(offsets[:, slot // STRIPE : (slot + step) // STRIPE]),
+                    in0=y[:, lo : lo + step],
+                    in1=gates[:, slot : slot + step],
+                    op=MULT,
                 )
 
-        def late_gathers(lo, hi):
-            gather(g_words[:, PASSES - 1, :], x_words[PASSES - 1], lo, hi)
-            gather(g_scales, x_scales, lo, hi)
-
-        late_gathers(0, 1024)
+        for lo in range(0, E * C, 1024):
+            gather(g_scales[:, lo : lo + 1024], x_scales, lo, lo + 1024)
+        late = [late_words(0), late_words(1), late_words(2)]
         weights(0)
+        y0 = multiply(0, late[0])
         weights(1)
-        z0 = multiply(0)
-        z1 = multiply(1)
-        late_gathers(1024, 2048)
-        scatter(0, z0)
+        late.append(late_words(3))
+        y1 = multiply(1, late[1])
+        scatter(0, y0, C)
         weights(2)
-        z2 = multiply(2)
-        scatter(1, z1)
+        y2 = multiply(2, late[2])
+        scatter(1, y1, 2 * C)
         weights(3)
-        z3 = multiply(3)
-        scatter(2, z2)
-        scatter(3, z3)
+        y3 = multiply(3, late[3])
+        scatter(2, y2, 2 * C)
+        scatter(3, y3, C)
         nc.sync.dma_start(out=out, in_=window[:])

@@ -20,8 +20,14 @@ MULT = mybir.AluOpType.mult
 SILU = mybir.ActivationFunctionType.Silu
 
 HALF = 1024
-LOADS = ((SUB, SUB), (HALF,), (HALF,), (HALF,), (HALF,), (SUB, SUB))
-SCALAR_TOKENS = ((512, 0, 512, 0), (512, 256, 512, 256), (512, 128, 256, 160))
+LOADS = (
+    (((512, 512),), ((512, 256),)),
+    (((512, 512), (512, 320)),),
+    (((512, 512), (512, 384)),),
+    (((512, 320),), ((512, 256),)),
+    (((512, 512), (512, 384)),),
+    (((512, 352),), ((256, 128),), ((256, 96),)),
+)
 
 
 def tile_routed_moe_kernel(tc, xT, w, b, gate, offs, out):
@@ -35,21 +41,19 @@ def tile_routed_moe_kernel(tc, xT, w, b, gate, offs, out):
 
     with (
         tc.tile_pool(name="keep", bufs=1) as keep,
-        tc.tile_pool(name="raw", bufs=6) as raw_pool,
+        tc.tile_pool(name="raw", bufs=1) as raw_pool,
         tc.tile_pool(name="group", bufs=4) as group_pool,
-        tc.tile_pool(name="wgroup", bufs=2) as wgroup_pool,
-        tc.tile_pool(name="late", bufs=3) as late_pool,
-        tc.tile_pool(name="ys", bufs=3) as y_pool,
+        tc.tile_pool(name="wgroup", bufs=3) as wgroup_pool,
         tc.psum_pool(name="psum", bufs=8) as psum_pool,
     ):
         offsets = keep.tile([P, E * C // STRIPE], U16, name="offsets")
         bias = keep.tile([P, E], F32, name="bias")
-        gates = keep.tile([P, E * C], F32, name="gates")
         window = keep.tile([P, T], F32, name="window")
         x_words = [keep.tile([P, T], U32, name=f"x_words{a}", align_bytes=64) for a in range(PASSES)]
         x_scales = keep.tile([P, T], U8, name="x_scales", align_bytes=64)
-        g_words = keep.tile([P, PASSES - 1, E * C], U32, name="g_words", align_bytes=64)
-        g_scales = keep.tile([P, E * C], U8, name="g_scales", align_bytes=64)
+        g_words = keep.tile([P, PASSES, E * C], U32, name="g_words", align_bytes=64)
+        gates = keep.tile([P, E * C], F32, name="gates")
+        g_scales_0 = keep.tile([P, HALF], U8, name="g_scales_0", align_bytes=64)
         w_words = keep.tile([P, E, PASSES, N], U32, name="w_words", align_bytes=64)
         w_scales = keep.tile([P, E, PASSES, N], U8, name="w_scales", align_bytes=64)
         warm = keep.tile([P, 1], F32, name="warm")
@@ -66,42 +70,42 @@ def tile_routed_moe_kernel(tc, xT, w, b, gate, offs, out):
             planes = xT[a * K_PASS : (a + 1) * K_PASS, :].rearrange("(p t) n -> p t n", t=PACK)
             for half in range(T // HALF):
                 t0 = half * HALF
-                raw = raw_pool.tile([P, PACK, HALF], F32, name="raw", tag="raw")
+                raw = raw_pool.tile([P, PACK, HALF], F32, name="raw", tag=f"raw{2 * a + half}", align_bytes=64)
+                pieces = []
                 c0 = 0
-                for width in LOADS[2 * a + half]:
+                for load in LOADS[2 * a + half]:
+                    width = sum(tokens for tokens, split in load)
                     nc.sync.dma_start(out=raw[:, :, c0 : c0 + width], in_=planes[:, :, t0 + c0 : t0 + c0 + width])
-                    c0 += width
+                    for tokens, split in load:
+                        pieces.append((c0, tokens, split))
+                        c0 += tokens
                 if first:
                     nc.sync.dma_start(out=offsets[:], in_=offs)
                     nc.sync.dma_start(out=bias[:], in_=b)
                     first = False
-                for s in range(0, HALF, SUB):
-                    grouped = group_pool.tile([P, SUB, PACK], BF16, name="grouped", align_bytes=64)
-                    split = SCALAR_TOKENS[a][(t0 + s) // SUB]
-                    if split > 0:
-                        interleave(nc.scalar.copy, grouped[:, :split, :], raw[:, :, s : s + split])
-                    if split < SUB:
-                        interleave(nc.vector.tensor_copy, grouped[:, split:, :], raw[:, :, s + split : s + SUB])
+                for s, tokens, split in pieces:
+                    grouped = group_pool.tile([P, tokens, PACK], BF16, name="grouped", align_bytes=64)
+                    interleave(nc.scalar.copy, grouped[:, :split, :], raw[:, :, s : s + split])
+                    if split < tokens:
+                        interleave(nc.vector.tensor_copy, grouped[:, split:, :], raw[:, :, s + split : s + tokens])
                     nc.vector.quantize_mx(
-                        out=x_words[a][:, t0 + s : t0 + s + SUB].bitcast(FP8X4),
-                        scales=x_scales[4 * a :, t0 + s : t0 + s + SUB],
+                        out=x_words[a][:, t0 + s : t0 + s + tokens].bitcast(FP8X4),
+                        scales=x_scales[4 * a :, t0 + s : t0 + s + tokens],
                         in_=grouped[:].rearrange("p c t -> p (c t)"),
                     )
-            if a < PASSES - 1:
-                for lo in range(0, E * C, 1024):
-                    gather(g_words[:, a, lo : lo + 1024], x_words[a], lo, lo + 1024)
+            for lo in range(0, E * C, 1024):
+                gather(g_words[:, a, lo : lo + 1024], x_words[a], lo, lo + 1024)
 
+        nc.sync.dma_start(out=gates[:], in_=gate)
         w_raws = []
         for pair in range(E // 2):
-            w_pair = raw_pool.tile([P, 2, PASSES, PACK, N], F32, name="w_pair", tag="raw")
+            w_pair = raw_pool.tile([P, 2, PASSES, PACK, N], F32, name="w_pair", tag=f"raw{pair}", align_bytes=64)
             for i in range(2):
                 nc.sync.dma_start(
                     out=w_pair[:, i].rearrange("p a t n -> p a (t n)"),
                     in_=w[2 * pair + i].rearrange("(a p t) n -> p a (t n)", p=P, t=PACK),
                 )
             w_raws.append(w_pair)
-            if pair == 1:
-                nc.sync.dma_start(out=gates[:], in_=gate)
 
         def weights(pair):
             experts = slice(2 * pair, 2 * pair + 2)
@@ -118,30 +122,25 @@ def tile_routed_moe_kernel(tc, xT, w, b, gate, offs, out):
                     out=words[:, lo:hi].bitcast(FP8X4), scales=scales[:, lo:hi], in_=values[:, PACK * lo : PACK * hi]
                 )
 
-        def late_words(pair):
-            words = late_pool.tile([P, 2 * C], U32, name="late", align_bytes=64)
-            gather(words[:], x_words[PASSES - 1], pair * 2 * C, (pair + 1) * 2 * C)
-            return words
-
-        def multiply(pair, late):
-            y = y_pool.tile([P, 2 * C], F32, name="y")
+        def multiply(pair):
+            y = raw_pool.tile([P, 2 * C], F32, name="y", tag=f"raw{pair + 1}", align_bytes=64)
+            scales = g_scales[pair // 2]
+            base = (pair // 2) * HALF
             for i in range(2):
                 e = 2 * pair + i
                 slots = slice(e * C, (e + 1) * C)
-                here = slice(i * C, (i + 1) * C)
                 acc = psum_pool.tile([P, C], F32, name="acc")
                 for a in range(PASSES):
-                    words = late[:, here] if a == PASSES - 1 else g_words[:, a, slots]
                     nc.tensor.matmul_mx(
                         out=acc[:],
                         lhsT=w_words[:, e, a, :].bitcast(FP8X4),
                         lhsT_scale=w_scales[:, e, a, :],
-                        rhs=words.bitcast(FP8X4),
-                        rhs_scale=g_scales[4 * a :, slots],
+                        rhs=g_words[:, a, slots].bitcast(FP8X4),
+                        rhs_scale=scales[4 * a :, e * C - base : (e + 1) * C - base],
                         start=(a == 0),
                         stop=(a == PASSES - 1),
                     )
-                nc.scalar.activation(out=y[:, here], in_=acc[:], func=SILU, bias=bias[:, e : e + 1])
+                nc.scalar.activation(out=y[:, i * C : (i + 1) * C], in_=acc[:], func=SILU, bias=bias[:, e : e + 1])
             return y
 
         def scatter(pair, y, step):
@@ -154,20 +153,18 @@ def tile_routed_moe_kernel(tc, xT, w, b, gate, offs, out):
                     op=MULT,
                 )
 
-        for lo in range(0, E * C, 1024):
-            gather(g_scales[:, lo : lo + 1024], x_scales, lo, lo + 1024)
-        late = [late_words(0), late_words(1), late_words(2)]
+        gather(g_scales_0[:], x_scales, 0, HALF)
         weights(0)
-        y0 = multiply(0, late[0])
+        g_scales_1 = raw_pool.tile([P, HALF], U8, name="g_scales_1", tag="raw0", align_bytes=64)
+        gather(g_scales_1[:], x_scales, HALF, 2 * HALF)
+        g_scales = (g_scales_0, g_scales_1)
         weights(1)
-        late.append(late_words(3))
-        y1 = multiply(1, late[1])
-        scatter(0, y0, C)
+        ys = [multiply(0)]
         weights(2)
-        y2 = multiply(2, late[2])
-        scatter(1, y1, 2 * C)
+        ys.append(multiply(1))
         weights(3)
-        y3 = multiply(3, late[3])
-        scatter(2, y2, 2 * C)
-        scatter(3, y3, C)
+        ys.append(multiply(2))
+        ys.append(multiply(3))
+        for pair in range(E // 2):
+            scatter(pair, ys[pair], 2 * C)
         nc.sync.dma_start(out=out, in_=window[:])

@@ -21,13 +21,15 @@ SILU = mybir.ActivationFunctionType.Silu
 
 HALF = 1024
 LOADS = (
-    (((512, 512),), ((512, 256),)),
-    (((512, 512), (512, 320)),),
-    (((512, 512), (512, 384)),),
-    (((512, 320),), ((512, 256),)),
-    (((512, 512), (512, 384)),),
-    (((512, 352),), ((256, 128),), ((256, 96),)),
+    (((512, 288), (512, 448)),),
+    (((512, 64), (512, 384)),),
+    (((512, 480), (512, 448)),),
+    (((512, 160), (512, 352)),),
+    (((512, 512),), ((512, 480),)),
+    (((512, 416),), ((256, 192),), ((256, 128),)),
 )
+W_SLOTS = (0, 1, 3, 4)
+Y_SLOTS = (1, 3, 4, 5)
 
 
 def tile_routed_moe_kernel(tc, xT, w, b, gate, offs, out):
@@ -52,7 +54,6 @@ def tile_routed_moe_kernel(tc, xT, w, b, gate, offs, out):
         x_words = [keep.tile([P, T], U32, name=f"x_words{a}", align_bytes=64) for a in range(PASSES)]
         x_scales = keep.tile([P, T], U8, name="x_scales", align_bytes=64)
         g_words = keep.tile([P, PASSES, E * C], U32, name="g_words", align_bytes=64)
-        gates = keep.tile([P, E * C], F32, name="gates")
         g_scales_0 = keep.tile([P, HALF], U8, name="g_scales_0", align_bytes=64)
         w_words = keep.tile([P, E, PASSES, N], U32, name="w_words", align_bytes=64)
         w_scales = keep.tile([P, E, PASSES, N], U8, name="w_scales", align_bytes=64)
@@ -81,7 +82,6 @@ def tile_routed_moe_kernel(tc, xT, w, b, gate, offs, out):
                         c0 += tokens
                 if first:
                     nc.sync.dma_start(out=offsets[:], in_=offs)
-                    nc.sync.dma_start(out=bias[:], in_=b)
                     first = False
                 for s, tokens, split in pieces:
                     grouped = group_pool.tile([P, tokens, PACK], BF16, name="grouped", align_bytes=64)
@@ -96,24 +96,28 @@ def tile_routed_moe_kernel(tc, xT, w, b, gate, offs, out):
             for lo in range(0, E * C, 1024):
                 gather(g_words[:, a, lo : lo + 1024], x_words[a], lo, lo + 1024)
 
-        nc.sync.dma_start(out=gates[:], in_=gate)
+        nc.sync.dma_start(out=bias[:], in_=b)
         w_raws = []
         for pair in range(E // 2):
-            w_pair = raw_pool.tile([P, 2, PASSES, PACK, N], F32, name="w_pair", tag=f"raw{pair}", align_bytes=64)
+            w_pair = raw_pool.tile([P, 2, PASSES, PACK, N], F32, name="w_pair", tag=f"raw{W_SLOTS[pair]}", align_bytes=64)
             for i in range(2):
                 nc.sync.dma_start(
                     out=w_pair[:, i].rearrange("p a t n -> p a (t n)"),
                     in_=w[2 * pair + i].rearrange("(a p t) n -> p a (t n)", p=P, t=PACK),
                 )
             w_raws.append(w_pair)
+            if pair == 1:
+                gates = raw_pool.tile([P, E * C], F32, name="gates", tag="raw2", align_bytes=64)
+                nc.sync.dma_start(out=gates[:], in_=gate)
 
         def weights(pair):
             experts = slice(2 * pair, 2 * pair + 2)
             grouped = wgroup_pool.tile([P, 2 * PASSES, N, PACK], BF16, name="w_grouped", align_bytes=64)
-            nc.scalar.copy(
-                out=grouped[:].rearrange("p a (c i) t -> p a c t i", i=4),
-                in_=w_raws[pair][:].rearrange("p e a t (c i) -> p (e a) c t i", i=4),
-            )
+            for i in range(2):
+                nc.scalar.copy(
+                    out=grouped[:, i * PASSES : (i + 1) * PASSES].rearrange("p a (c i) t -> p a c t i", i=4),
+                    in_=w_raws[pair][:, i].rearrange("p a t (c i) -> p a c t i", i=4),
+                )
             words = w_words[:, experts].rearrange("p e a n -> p (e a n)")
             scales = w_scales[:, experts].rearrange("p e a n -> p (e a n)")
             values = grouped[:].rearrange("p a n t -> p (a n t)")
@@ -123,7 +127,7 @@ def tile_routed_moe_kernel(tc, xT, w, b, gate, offs, out):
                 )
 
         def multiply(pair):
-            y = raw_pool.tile([P, 2 * C], F32, name="y", tag=f"raw{pair + 1}", align_bytes=64)
+            y = raw_pool.tile([P, 2 * C], F32, name="y", tag=f"raw{Y_SLOTS[pair]}", align_bytes=64)
             scales = g_scales[pair // 2]
             base = (pair // 2) * HALF
             for i in range(2):

import concourse.mybir as mybir

K, T, E, C, N = 1536, 2048, 8, 256, 128
FLOPS = 2 * K * E * C * N

P = 128
PACK = 4
K_PASS = P * PACK
PASSES = K // K_PASS
SUB = 512
STRIPE = 16

F32 = mybir.dt.float32
BF16 = mybir.dt.bfloat16
U32 = mybir.dt.uint32
U16 = mybir.dt.uint16
U8 = mybir.dt.uint8
FP8X4 = mybir.dt.float8_e4m3fn_x4
MULT = mybir.AluOpType.mult
SILU = mybir.ActivationFunctionType.Silu

HALF = 1024
LOADS = (
    (((512, 288), (512, 448)),),
    (((512, 64), (512, 384)),),
    (((512, 480), (512, 448)),),
    (((512, 160), (512, 352)),),
    (((512, 512),), ((512, 480),)),
    (((512, 416),), ((256, 192),), ((256, 128),)),
)
W_SLOTS = (0, 1, 3, 4)
Y_SLOTS = (1, 3, 4, 5)


def tile_routed_moe_kernel(tc, xT, w, b, gate, offs, out):
    nc = tc.nc

    def interleave(engine_copy, dst, src):
        engine_copy(
            out=dst.rearrange("p (c i) t -> p c t i", i=4),
            in_=src.rearrange("p t (c i) -> p c t i", i=4),
        )

    with (
        tc.tile_pool(name="keep", bufs=1) as keep,
        tc.tile_pool(name="raw", bufs=1) as raw_pool,
        tc.tile_pool(name="group", bufs=4) as group_pool,
        tc.tile_pool(name="wgroup", bufs=3) as wgroup_pool,
        tc.psum_pool(name="psum", bufs=8) as psum_pool,
    ):
        offsets = keep.tile([P, E * C // STRIPE], U16, name="offsets")
        bias = keep.tile([P, E], F32, name="bias")
        window = keep.tile([P, T], F32, name="window")
        x_words = [keep.tile([P, T], U32, name=f"x_words{a}", align_bytes=64) for a in range(PASSES)]
        x_scales = keep.tile([P, T], U8, name="x_scales", align_bytes=64)
        g_words = keep.tile([P, PASSES, E * C], U32, name="g_words", align_bytes=64)
        g_scales_0 = keep.tile([P, HALF], U8, name="g_scales_0", align_bytes=64)
        w_words = keep.tile([P, E, PASSES, N], U32, name="w_words", align_bytes=64)
        w_scales = keep.tile([P, E, PASSES, N], U8, name="w_scales", align_bytes=64)
        warm = keep.tile([P, 1], F32, name="warm")

        nc.gpsimd.memset(x_scales[:], 0)
        nc.gpsimd.memset(warm[:], 0.0)
        nc.scalar.activation(out=warm[:], in_=warm[:], func=SILU)

        def gather(dst, src, lo, hi):
            nc.vector.tensor_copy(out=dst, in_=src[:].indirect(offsets[:, lo // STRIPE : hi // STRIPE]))

        first = True
        for a in range(PASSES):
            planes = xT[a * K_PASS : (a + 1) * K_PASS, :].rearrange("(p t) n -> p t n", t=PACK)
            for half in range(T // HALF):
                t0 = half * HALF
                raw = raw_pool.tile([P, PACK, HALF], F32, name="raw", tag=f"raw{2 * a + half}", align_bytes=64)
                pieces = []
                c0 = 0
                for load in LOADS[2 * a + half]:
                    width = sum(tokens for tokens, split in load)
                    nc.sync.dma_start(out=raw[:, :, c0 : c0 + width], in_=planes[:, :, t0 + c0 : t0 + c0 + width])
                    for tokens, split in load:
                        pieces.append((c0, tokens, split))
                        c0 += tokens
                if first:
                    nc.sync.dma_start(out=offsets[:], in_=offs)
                    first = False
                for s, tokens, split in pieces:
                    grouped = group_pool.tile([P, tokens, PACK], BF16, name="grouped", align_bytes=64)
                    interleave(nc.scalar.copy, grouped[:, :split, :], raw[:, :, s : s + split])
                    if split < tokens:
                        interleave(nc.vector.tensor_copy, grouped[:, split:, :], raw[:, :, s + split : s + tokens])
                    nc.vector.quantize_mx(
                        out=x_words[a][:, t0 + s : t0 + s + tokens].bitcast(FP8X4),
                        scales=x_scales[4 * a :, t0 + s : t0 + s + tokens],
                        in_=grouped[:].rearrange("p c t -> p (c t)"),
                    )
            for lo in range(0, E * C, 1024):
                gather(g_words[:, a, lo : lo + 1024], x_words[a], lo, lo + 1024)

        nc.sync.dma_start(out=bias[:], in_=b)
        w_raws = []
        for pair in range(E // 2):
            w_pair = raw_pool.tile([P, 2, PASSES, PACK, N], F32, name="w_pair", tag=f"raw{W_SLOTS[pair]}", align_bytes=64)
            for i in range(2):
                nc.sync.dma_start(
                    out=w_pair[:, i].rearrange("p a t n -> p a (t n)"),
                    in_=w[2 * pair + i].rearrange("(a p t) n -> p a (t n)", p=P, t=PACK),
                )
            w_raws.append(w_pair)
            if pair == 1:
                gates = raw_pool.tile([P, E * C], F32, name="gates", tag="raw2", align_bytes=64)
                nc.sync.dma_start(out=gates[:], in_=gate)

        def weights(pair):
            experts = slice(2 * pair, 2 * pair + 2)
            grouped = wgroup_pool.tile([P, 2 * PASSES, N, PACK], BF16, name="w_grouped", align_bytes=64)
            for i in range(2):
                nc.scalar.copy(
                    out=grouped[:, i * PASSES : (i + 1) * PASSES].rearrange("p a (c i) t -> p a c t i", i=4),
                    in_=w_raws[pair][:, i].rearrange("p a t (c i) -> p a c t i", i=4),
                )
            words = w_words[:, experts].rearrange("p e a n -> p (e a n)")
            scales = w_scales[:, experts].rearrange("p e a n -> p (e a n)")
            values = grouped[:].rearrange("p a n t -> p (a n t)")
            for lo, hi in ((0, 4 * N), (4 * N, 6 * N)):
                nc.vector.quantize_mx(
                    out=words[:, lo:hi].bitcast(FP8X4), scales=scales[:, lo:hi], in_=values[:, PACK * lo : PACK * hi]
                )

        def multiply(pair):
            y = raw_pool.tile([P, 2 * C], F32, name="y", tag=f"raw{Y_SLOTS[pair]}", align_bytes=64)
            scales = g_scales[pair // 2]
            base = (pair // 2) * HALF
            for i in range(2):
                e = 2 * pair + i
                slots = slice(e * C, (e + 1) * C)
                acc = psum_pool.tile([P, C], F32, name="acc")
                for a in range(PASSES):
                    nc.tensor.matmul_mx(
                        out=acc[:],
                        lhsT=w_words[:, e, a, :].bitcast(FP8X4),
                        lhsT_scale=w_scales[:, e, a, :],
                        rhs=g_words[:, a, slots].bitcast(FP8X4),
                        rhs_scale=scales[4 * a :, e * C - base : (e + 1) * C - base],
                        start=(a == 0),
                        stop=(a == PASSES - 1),
                    )
                nc.scalar.activation(out=y[:, i * C : (i + 1) * C], in_=acc[:], func=SILU, bias=bias[:, e : e + 1])
            return y

        def scatter(pair, y, step):
            for lo in range(0, 2 * C, step):
                slot = pair * 2 * C + lo
                nc.vector.tensor_tensor(
                    out=window[:].indirect(offsets[:, slot // STRIPE : (slot + step) // STRIPE]),
                    in0=y[:, lo : lo + step],
                    in1=gates[:, slot : slot + step],
                    op=MULT,
                )

        gather(g_scales_0[:], x_scales, 0, HALF)
        weights(0)
        g_scales_1 = raw_pool.tile([P, HALF], U8, name="g_scales_1", tag="raw0", align_bytes=64)
        gather(g_scales_1[:], x_scales, HALF, 2 * HALF)
        g_scales = (g_scales_0, g_scales_1)
        weights(1)
        ys = [multiply(0)]
        weights(2)
        ys.append(multiply(1))
        weights(3)
        ys.append(multiply(2))
        ys.append(multiply(3))
        for pair in range(E // 2):
            scatter(pair, ys[pair], 2 * C)
        nc.sync.dma_start(out=out, in_=window[:])
